import numpy as np
import ml_dtypes


def mxq(x, axis, fmt="e4m3"):
    dtype, down = {"e4m3": (ml_dtypes.float8_e4m3fn, 7), "e5m2": (ml_dtypes.float8_e5m2, 14)}[fmt]
    v = np.moveaxis(np.asarray(x, np.float32).astype(ml_dtypes.bfloat16).astype(np.float64), axis, -1)
    blocks = v.reshape(v.shape[:-1] + (-1, 32))
    amax = np.abs(blocks).max(-1, keepdims=True)
    byte = np.maximum(np.where(amax > 0, np.frexp(amax)[1] - 1 + 127, 0) - down, 1)
    scale = np.exp2(byte - 127.0)
    codes = (blocks / scale).astype(np.float32).astype(dtype).astype(np.float64)
    return np.moveaxis((codes * scale).reshape(v.shape), -1, axis)


WIDE = False


def mx_kscale(k):
    if not WIDE:
        return np.ones(k)
    levels = np.array([10, -10, 5, -5, 0])
    if k % 512:
        return np.exp2(np.random.permutation(np.resize(levels, k // 32))).repeat(32)
    a = np.empty((k // 512, 16))
    for p in range(k // 512):
        a[p, :8] = np.random.permutation(np.resize(levels, 8))
        for g in range(8):
            far = levels[np.abs(levels - a[p, g]) >= 10]
            a[p, g + 8] = far[np.random.randint(len(far))]
    return np.exp2(a.ravel()).repeat(32)


def f64(x):
    return np.asarray(x).astype(np.float64)


def striped(idx):
    return np.tile(idx.reshape(-1, 16).T, (8, 1)).astype(np.uint16)


def unstriped(offs):
    return offs[:16].T.reshape(-1).astype(np.int64)


def striped8(idx):
    return np.concatenate([x.reshape(-1, 16).T for x in idx]).astype(np.uint16)


def runs(offs, k):
    lists = np.stack([offs[16 * r : 16 * r + 16].T.reshape(-1) for r in range(8)]).astype(np.int64)
    return lists[np.arange(k) % 512 // 64]


def pack_weight(w):
    k, n = w.shape
    w = f64(np.asarray(w, np.float32).astype(ml_dtypes.bfloat16)).reshape(k // 32, 32, n)
    amax = np.abs(w).max(1)
    byte = np.clip(np.where(amax > 0, np.frexp(amax)[1] - 1 + 127 - 7, 1), 1, 254)
    scaled = (w * np.exp2(127.0 - byte)[:, None, :]).reshape(k, n).astype(np.float32)
    words = np.ascontiguousarray(scaled.reshape(k // 512, 128, 4, n).transpose(0, 1, 3, 2)).astype(ml_dtypes.float8_e4m3fn).view(np.uint8)
    return words, np.ascontiguousarray(byte.astype(np.uint8).reshape(k // 512, 16, n))


def unpack_weight(words, scales):
    g, p, n, _ = words.shape
    vals = np.ascontiguousarray(words).view(ml_dtypes.float8_e4m3fn).astype(np.float64) * np.repeat(np.exp2(scales.astype(np.float64) - 127.0), 8, axis=1)[..., None]
    return vals.transpose(0, 1, 3, 2).reshape(g * 512, n)


K, T, S, V, N, H = 512, 2048, 1024, 512, 512, 512


def setup_inputs():
    n = np.random.standard_normal
    s = mx_kscale(K)[:, None]
    u = mx_kscale(H)
    packed_xT = pack_weight(n((K, T)) * s)
    return {
        "x_words": packed_xT[0],
        "x_scales": packed_xT[1],
        "w1": (n((K, H)) / np.sqrt(K) / s).astype(np.float32),
        "gn": (np.random.uniform(0.5, 1.5, (H, 1)) * u[:, None]).astype(np.float32),
        "w2": (n((H, N)) / np.sqrt(H) / u[:, None]).astype(np.float32),
        "offs": striped(np.random.permutation(T)[:S]),
        "n1": striped8(np.stack([np.random.permutation(S) for _ in range(8)])),
        "n2": striped8(np.stack([np.random.permutation(V) for _ in range(8)])),
        "n3": striped8(np.stack([np.random.permutation(V) for _ in range(8)])),
        "n4": striped8(np.stack([np.random.permutation(V) for _ in range(8)])),
    }


def reference(x_words, x_scales, w1, gn, w2, offs, n1, n2, n3, n4):
    xq = unpack_weight(x_words, x_scales)[:, unstriped(offs)]
    y = mxq(f64(w1), 0, "e4m3").T @ xq
    ln = y[np.arange(H)[:, None], runs(n1, H)]
    mx = ln.reshape(H, V, 2).max(axis=2)
    mn = ln.reshape(H, V, 2).min(axis=2)
    z = f64(gn) * (mx - (0.5 * mn))
    h = mxq(f64(w2), 0, "e4m3").T @ mxq(z, 0, "e4m3")
    b1 = h[np.arange(N)[:, None], runs(n2, N)]
    b2 = h[np.arange(N)[:, None], runs(n3, N)]
    b3 = h[np.arange(N)[:, None], runs(n4, N)]
    return np.maximum(np.maximum(b1, b2), b3) - (0.5 * (np.maximum(np.minimum(b1, b2), np.minimum(np.maximum(b1, b2), b3))))

@@ -1,0 +1,222 @@
+from contextlib import ExitStack
+
+import concourse.mybir as mybir
+from concourse.masks import make_identity
+
+K, T, S, V, H, N = 512, 2048, 1024, 512, 512, 512
+FLOPS = 2 * K * H * S + 2 * H * N * V
+
+F32 = mybir.dt.float32
+BF16 = mybir.dt.bfloat16
+I32 = mybir.dt.int32
+U32 = mybir.dt.uint32
+U16 = mybir.dt.uint16
+U8 = mybir.dt.uint8
+FP8X4 = mybir.dt.float8_e4m3fn_x4
+ALU = mybir.AluOpType
+ACT = mybir.ActivationFunctionType
+
+P = 128
+PACK = 4
+BANK = 512
+
+
+def tile_picked_laypgaptop2_none_p_kernel(tc, x_words, x_scales, w1, gn, w2, offs, n1, n2, n3, n4, out):
+    nc = tc.nc
+    with ExitStack() as ctx:
+        keep = ctx.enter_context(tc.tile_pool(name="keep", bufs=1))
+        ring = ctx.enter_context(tc.tile_pool(name="ring", bufs=3))
+        psum = ctx.enter_context(tc.psum_pool(name="psum", bufs=1))
+
+        def load_list(src, name):
+            lst = keep.tile(list(src.shape), U16, name=name)
+            nc.sync.dma_start(lst[:], src)
+            return lst
+
+        def entries(lst, first, count):
+            return lst[:, first // 16 : (first + count) // 16]
+
+        scale_tab = keep.tile([P, T], U8, name="scale_tab")
+        nc.vector.memset(scale_tab[:].bitcast(I32), 0)
+        offs_l = load_list(offs, "offs_l")
+        gain = keep.tile([P, PACK], F32, name="gain")
+        nc.sync.dma_start(gain[:], gn.rearrange("(p t) o -> p (t o)", t=PACK))
+        for q in range(4):
+            nc.sync.dma_start(scale_tab[32 * q : 32 * q + 4, :].bitcast(I32), x_scales[0, 4 * q : 4 * q + 4, :].bitcast(I32))
+        word_tab = keep.tile([P, T], I32, name="word_tab")
+        nc.sync.dma_start(word_tab[:], x_words[0].rearrange("p n t -> p (n t)").bitcast(I32))
+
+        def load_weight(w, name):
+            halves = []
+            for c in range(2):
+                raw = keep.tile([P, PACK, 256], F32, name="%s_raw%d" % (name, c))
+                nc.sync.dma_start(raw[:], w.rearrange("(p j) c -> p j c", j=PACK)[:, :, 256 * c : 256 * (c + 1)])
+                halves.append(raw)
+            return halves
+
+        w1_raw = load_weight(w1, "w1")
+        n1_l = load_list(n1, "n1_l")
+        w2_raw = load_weight(w2, "w2")
+        n2_l = load_list(n2, "n2_l")
+        n3_l = load_list(n3, "n3_l")
+        n4_l = load_list(n4, "n4_l")
+
+        ident = keep.tile([P, P], F32, name="ident")
+        make_identity(nc, ident[:])
+        gain4 = keep.tile([P, PACK], F32, name="gain4")
+        nc.scalar.activation(gain4[:], gain[:], ACT.Copy, scale=4.0)
+
+        x_scale = keep.tile([P, S], U8, name="x_scale", align_bytes=64)
+        nc.vector.tensor_copy(x_scale[:], scale_tab[:].indirect(offs_l[:]))
+        x_code = []
+        for c in range(2):
+            codes = keep.tile([P, BANK], U32, name="x_code%d" % c, align_bytes=64)
+            nc.vector.tensor_copy(codes[:], word_tab[:].bitcast(U32).indirect(entries(offs_l, BANK * c, BANK)))
+            x_code.append(codes)
+
+        def deal_views(grouped, raw, c):
+            dst = grouped[:].rearrange("p (t m j) -> p m j t", t=PACK, j=PACK)[:, 64 * c : 64 * (c + 1)]
+            return dst, raw[:].rearrange("p j (m t) -> p m j t", t=PACK)
+
+        def quantise(grouped, first, width, name):
+            codes = keep.tile([P, width // PACK], U32, name=name + "_code", align_bytes=64)
+            scales = keep.tile([P, width // PACK], U8, name=name + "_scale", align_bytes=64)
+            nc.vector.quantize_mx(out=codes[:].bitcast(FP8X4), scales=scales[:], in_=grouped[:, first : first + width])
+            return codes, scales
+
+        w1_b = keep.tile([P, PACK * H], BF16, name="w1_b", align_bytes=64)
+        nc.scalar.copy(*deal_views(w1_b, w1_raw[0], 0))
+        nc.vector.tensor_copy(*deal_views(w1_b, w1_raw[1], 1))
+        w1_q = [quantise(w1_b, 512 * t, 512, "w1q%d" % t) for t in range(PACK)]
+
+        y = [keep.tile([P, S], F32, name="y%d" % t) for t in range(PACK)]
+        for t in range(PACK):
+            for c in range(2):
+                acc = psum.tile([P, BANK], F32, name="acc", tag="mm", bufs=3)
+                nc.tensor.matmul_mx(out=acc[:], lhsT=w1_q[t][0][:].bitcast(FP8X4), lhsT_scale=w1_q[t][1][:],
+                                    rhs=x_code[c][:].bitcast(FP8X4), rhs_scale=x_scale[:, BANK * c : BANK * (c + 1)], start=True, stop=True)
+                nc.scalar.activation(y[t][:, BANK * c : BANK * (c + 1)], acc[:], ACT.Copy, scale=0.25)
+
+        def add_turned(dst, terms):
+            for i, term in enumerate(terms):
+                nc.tensor.matmul(dst, term, ident[:], is_transpose=True, start=(i == 0), stop=(i == len(terms) - 1))
+
+        def turn_back(turned, blocks):
+            staged = ring.tile([P, blocks * P], F32, name="staged", tag="staged")
+            nc.scalar.copy(staged[:], turned[:, : blocks * P])
+            back = psum.tile([P, BANK], F32, name="back", tag="back", bufs=2)
+            for b in range(blocks):
+                nc.tensor.transpose(back[:, P * b : P * (b + 1)], staged[:, P * b : P * (b + 1)], ident[:])
+            return back
+
+        def line_up(dst, t, v0, n):
+            nc.vector.tensor_copy(dst, y[t][:].indirect(entries(n1_l, 2 * v0, 2 * n)))
+
+        def gap_term(lined, n):
+            diff = ring.tile([P, n], F32, name="diff", tag="diff")
+            nc.vector.tensor_tensor(diff[:], lined[:, 0::2], lined[:, 1::2], ALU.subtract)
+            gap = keep.tile([P, n], F32, name="gap", tag="gap", bufs=5)
+            nc.scalar.activation(gap[:], diff[:], ACT.Abs, scale=3.0)
+            return gap
+
+        def gained(z_b, src, g):
+            nc.vector.tensor_tensor(z_b.rearrange("p (v t) -> p v t", t=PACK), src.rearrange("p (t v) -> p v t", t=PACK),
+                                    g[:].unsqueeze(1).to_broadcast([P, P, PACK]), ALU.mult)
+
+        h = [keep.tile([P, V], F32, name="h%d" % t) for t in range(PACK)]
+
+        def second_product(z_q, v0, n):
+            for t in range(PACK):
+                acc = psum.tile([P, BANK], F32, name="acc", tag="mm", bufs=3)
+                nc.tensor.matmul_mx(out=acc[:, :n], lhsT=w2_q[0][:, P * t : P * (t + 1)].bitcast(FP8X4), lhsT_scale=w2_q[1][:, P * t : P * (t + 1)],
+                                    rhs=z_q[0][:].bitcast(FP8X4), rhs_scale=z_q[1][:], start=True, stop=True)
+                nc.scalar.activation(h[t][:, v0 : v0 + n], acc[:, :n], ACT.Copy, scale=-0.5)
+
+        turned0 = [psum.tile([P, BANK], F32, name="turned", tag="turned", bufs=3) for b in range(2)]
+        for t in range(PACK):
+            lined = keep.tile([P, 512], F32, name="lined0_%d" % t)
+            line_up(lined[:], t, 0, 256)
+            gap = gap_term(lined, 256)
+            for b in range(2):
+                add_turned(turned0[b][:, P * t : P * (t + 1)],
+                           [lined[:, 256 * b : 256 * (b + 1) : 2], lined[:, 256 * b + 1 : 256 * (b + 1) : 2], gap[:, P * b : P * (b + 1)]])
+        back0 = [turn_back(turned0[b], PACK) for b in range(2)]
+
+        w2_b = keep.tile([P, PACK * N], BF16, name="w2_b", align_bytes=64)
+        for c in range(2):
+            nc.scalar.copy(*deal_views(w2_b, w2_raw[c], c))
+
+        lined1 = keep.tile([P, 1024], F32, name="lined1")
+        for t in range(PACK):
+            line_up(lined1[:, 256 * t : 256 * (t + 1)], t, 256, P)
+        gap1 = gap_term(lined1, 512)
+        turned1 = psum.tile([P, BANK], F32, name="turned", tag="turned", bufs=3)
+        for t in range(PACK):
+            add_turned(turned1[:, P * t : P * (t + 1)],
+                       [lined1[:, 256 * t : 256 * (t + 1) : 2], lined1[:, 256 * t + 1 : 256 * (t + 1) : 2], gap1[:, P * t : P * (t + 1)]])
+        back1 = turn_back(turned1, PACK)
+
+        z0 = keep.tile([P, PACK * 256], BF16, name="z0", align_bytes=64)
+        for b in range(2):
+            gained(z0[:, 512 * b : 512 * (b + 1)], back0[b][:], gain)
+        w2_q = quantise(w2_b, 0, PACK * N, "w2q")
+        second_product(quantise(z0, 0, 1024, "z0q"), 0, 256)
+
+        lined2 = keep.tile([P, 1024], F32, name="lined2")
+        for t in range(PACK):
+            line_up(lined2[:, 256 * t : 256 * (t + 1)], t, 384, P)
+        larger = keep.tile([P, 512], F32, name="larger")
+        nc.vector.tensor_tensor(larger[:], lined2[:, 0::2], lined2[:, 1::2], ALU.max)
+        smaller = keep.tile([P, 512], F32, name="smaller")
+        nc.vector.tensor_tensor(smaller[:], lined2[:, 0::2], lined2[:, 1::2], ALU.min)
+        z1 = keep.tile([P, 512], BF16, name="z1", align_bytes=64)
+        gained(z1[:], back1[:], gain)
+        mixed = keep.tile([P, 512], F32, name="mixed")
+        nc.vector.scalar_tensor_tensor(mixed[:], smaller[:], -0.5, larger[:], ALU.mult, ALU.add)
+        z1_q = quantise(z1, 0, 512, "z1q")
+        z2 = keep.tile([P, 512], BF16, name="z2", align_bytes=64)
+        gained(z2[:], mixed[:], gain4)
+        second_product(z1_q, 256, P)
+        second_product(quantise(z2, 0, 512, "z2q"), 384, P)
+
+        out_rows = out.rearrange("(p t) v -> p t v", t=PACK)
+        W = 256
+        units = [(t, v0) for t in range(PACK) for v0 in range(0, V, W)]
+
+        def first_lookup(t, v0):
+            p1 = ring.tile([P, W], F32, name="p1", tag="p1")
+            nc.vector.tensor_scalar(p1[:], h[t][:].indirect(entries(n2_l, v0, W)), -1.0, 0.0, ALU.mult, ALU.add)
+            return p1
+
+        p1_next = first_lookup(*units[0])
+        for u, (t, v0) in enumerate(units):
+            p1 = p1_next
+            e2 = ring.tile([P, W], F32, name="e2", tag="e2")
+            nc.vector.tensor_tensor(e2[:], h[t][:].indirect(entries(n3_l, v0, W)), p1[:], ALU.add)
+            lift = ring.tile([P, W], F32, name="lift", tag="lift")
+            nc.scalar.activation(lift[:], e2[:], ACT.Relu, scale=-2.0)
+            e3 = ring.tile([P, W], F32, name="e3", tag="e3")
+            nc.vector.tensor_tensor(e3[:], h[t][:].indirect(entries(n4_l, v0, W)), p1[:], ALU.add)
+            if u + 1 < len(units):
+                p1_next = first_lookup(*units[u + 1])
+            over = ring.tile([P, W], F32, name="over", tag="over")
+            nc.vector.scalar_tensor_tensor(over[:], e2[:], 0.0, e3[:], ALU.min, ALU.subtract)
+            excess = ring.tile([P, W], F32, name="excess", tag="excess")
+            nc.scalar.activation(excess[:], over[:], ACT.Relu, scale=3.0)
+            second = ring.tile([P, W], F32, name="second", tag="second")
+            nc.vector.scalar_tensor_tensor(second[:], e2[:], 0.0, e3[:], ALU.max, ALU.min)
+            result = ring.tile([P, W], F32, name="result", tag="result")
+            if u + 1 < len(units):
+                turned = psum.tile([P, BANK], F32, name="turned", tag="turned", bufs=3)
+                for b in range(W // P):
+                    cols = slice(P * b, P * (b + 1))
+                    add_turned(turned[:, cols], [p1[:, cols], lift[:, cols], second[:, cols], excess[:, cols]])
+                back = turn_back(turned, W // P)
+                nc.scalar.copy(result[:], back[:, :W])
+            else:
+                part1 = keep.tile([P, W], F32, name="part1")
+                nc.vector.tensor_tensor(part1[:], p1[:], lift[:], ALU.add)
+                part2 = keep.tile([P, W], F32, name="part2")
+                nc.vector.tensor_tensor(part2[:], second[:], excess[:], ALU.add)
+                nc.vector.tensor_tensor(result[:], part1[:], part2[:], ALU.add)
+            nc.sync.dma_start(out_rows[:, t, v0 : v0 + W], result[:])

@@ -25,7 +25,6 @@ def tile_picked_laypgaptop2_none_p_kernel(tc, x_words, x_scales, w1, gn, w2, off
     nc = tc.nc
     with ExitStack() as ctx:
         keep = ctx.enter_context(tc.tile_pool(name="keep", bufs=1))
-        ring = ctx.enter_context(tc.tile_pool(name="ring", bufs=3))
         psum = ctx.enter_context(tc.psum_pool(name="psum", bufs=1))
 
         def load_list(src, name):
@@ -46,17 +45,13 @@ def tile_picked_laypgaptop2_none_p_kernel(tc, x_words, x_scales, w1, gn, w2, off
         word_tab = keep.tile([P, T], I32, name="word_tab")
         nc.sync.dma_start(word_tab[:], x_words[0].rearrange("p n t -> p (n t)").bitcast(I32))
 
-        def load_weight(w, name):
-            halves = []
-            for c in range(2):
-                raw = keep.tile([P, PACK, 256], F32, name="%s_raw%d" % (name, c))
-                nc.sync.dma_start(raw[:], w.rearrange("(p j) c -> p j c", j=PACK)[:, :, 256 * c : 256 * (c + 1)])
-                halves.append(raw)
-            return halves
+        def load_weight(w):
+            raw = keep.tile([P, PACK * 512], F32, name="w_raw", tag="w_raw", bufs=1)
+            nc.sync.dma_start(raw[:], w.rearrange("(p j) c -> p (j c)", j=PACK))
+            return raw
 
-        w1_raw = load_weight(w1, "w1")
+        w1_raw = load_weight(w1)
         n1_l = load_list(n1, "n1_l")
-        w2_raw = load_weight(w2, "w2")
         n2_l = load_list(n2, "n2_l")
         n3_l = load_list(n3, "n3_l")
         n4_l = load_list(n4, "n4_l")
@@ -74,20 +69,28 @@ def tile_picked_laypgaptop2_none_p_kernel(tc, x_words, x_scales, w1, gn, w2, off
             nc.vector.tensor_copy(codes[:], word_tab[:].bitcast(U32).indirect(entries(offs_l, BANK * c, BANK)))
             x_code.append(codes)
 
-        def deal_views(grouped, raw, c):
-            dst = grouped[:].rearrange("p (t m j) -> p m j t", t=PACK, j=PACK)[:, 64 * c : 64 * (c + 1)]
-            return dst, raw[:].rearrange("p j (m t) -> p m j t", t=PACK)
-
         def quantise(grouped, first, width, name):
             codes = keep.tile([P, width // PACK], U32, name=name + "_code", align_bytes=64)
             scales = keep.tile([P, width // PACK], U8, name=name + "_scale", align_bytes=64)
             nc.vector.quantize_mx(out=codes[:].bitcast(FP8X4), scales=scales[:], in_=grouped[:, first : first + width])
             return codes, scales
 
-        w1_b = keep.tile([P, PACK * H], BF16, name="w1_b", align_bytes=64)
-        nc.scalar.copy(*deal_views(w1_b, w1_raw[0], 0))
-        nc.vector.tensor_copy(*deal_views(w1_b, w1_raw[1], 1))
-        w1_q = [quantise(w1_b, 512 * t, 512, "w1q%d" % t) for t in range(PACK)]
+        w1_b = [keep.tile([P, 512], BF16, name="w1_b%d" % t, align_bytes=64) for t in range(PACK)]
+        w1_cols = w1_raw[:].rearrange("p (j m t) -> p t m j", j=PACK, t=PACK)
+
+        def deal_w1(copy, t):
+            copy(w1_b[t][:].rearrange("p (m j) -> p m j", j=PACK), w1_cols[:, t])
+
+        w1_q = [None] * PACK
+        deal_w1(nc.vector.tensor_copy, 0)
+        deal_w1(nc.scalar.copy, 1)
+        w1_q[0] = quantise(w1_b[0], 0, 512, "w1q0")
+        deal_w1(nc.vector.tensor_copy, 2)
+        w1_q[1] = quantise(w1_b[1], 0, 512, "w1q1")
+        deal_w1(nc.vector.tensor_copy, 3)
+        w1_q[2] = quantise(w1_b[2], 0, 512, "w1q2")
+        w1_q[3] = quantise(w1_b[3], 0, 512, "w1q3")
+        w2_raw = load_weight(w2)
 
         y = [keep.tile([P, S], F32, name="y%d" % t) for t in range(PACK)]
         for t in range(PACK):
@@ -101,8 +104,8 @@ def tile_picked_laypgaptop2_none_p_kernel(tc, x_words, x_scales, w1, gn, w2, off
             for i, term in enumerate(terms):
                 nc.tensor.matmul(dst, term, ident[:], is_transpose=True, start=(i == 0), stop=(i == len(terms) - 1))
 
-        def turn_back(turned, blocks):
-            staged = ring.tile([P, blocks * P], F32, name="staged", tag="staged")
+        def turn_back(turned, blocks, tag):
+            staged = keep.tile([P, blocks * P], F32, name="staged", tag=tag, bufs=1)
             nc.scalar.copy(staged[:], turned[:, : blocks * P])
             back = psum.tile([P, BANK], F32, name="back", tag="back", bufs=2)
             for b in range(blocks):
@@ -112,12 +115,10 @@ def tile_picked_laypgaptop2_none_p_kernel(tc, x_words, x_scales, w1, gn, w2, off
         def line_up(dst, t, v0, n):
             nc.vector.tensor_copy(dst, y[t][:].indirect(entries(n1_l, 2 * v0, 2 * n)))
 
-        def gap_term(lined, n):
-            diff = ring.tile([P, n], F32, name="diff", tag="diff")
+        def gap_term(gap, lined, n):
+            diff = keep.tile([P, n], F32, name="diff", tag="diff", bufs=5)
             nc.vector.tensor_tensor(diff[:], lined[:, 0::2], lined[:, 1::2], ALU.subtract)
-            gap = keep.tile([P, n], F32, name="gap", tag="gap", bufs=5)
-            nc.scalar.activation(gap[:], diff[:], ACT.Abs, scale=3.0)
-            return gap
+            nc.scalar.activation(gap, diff[:], ACT.Abs, scale=3.0)
 
         def gained(z_b, src, g):
             nc.vector.tensor_tensor(z_b.rearrange("p (v t) -> p v t", t=PACK), src.rearrange("p (t v) -> p v t", t=PACK),
@@ -132,91 +133,142 @@ def tile_picked_laypgaptop2_none_p_kernel(tc, x_words, x_scales, w1, gn, w2, off
                                     rhs=z_q[0][:].bitcast(FP8X4), rhs_scale=z_q[1][:], start=True, stop=True)
                 nc.scalar.activation(h[t][:, v0 : v0 + n], acc[:, :n], ACT.Copy, scale=-0.5)
 
+        w2_b = keep.tile([P, PACK * N], BF16, name="w2_b", align_bytes=64)
+
+        def deal_w2():
+            for c in range(4):
+                nc.scalar.copy(w2_b[:].rearrange("p (t m j) -> p m t j", t=PACK, j=PACK)[:, 32 * c : 32 * (c + 1)],
+                               w2_raw[:].rearrange("p (j m t) -> p m t j", j=PACK, t=PACK)[:, 32 * c : 32 * (c + 1)])
+
         turned0 = [psum.tile([P, BANK], F32, name="turned", tag="turned", bufs=3) for b in range(2)]
         for t in range(PACK):
             lined = keep.tile([P, 512], F32, name="lined0_%d" % t)
             line_up(lined[:], t, 0, 256)
-            gap = gap_term(lined, 256)
+            if t == 0:
+                gaps = keep.tile([P, 512], F32, name="gaps_early")
+            if t == 2:
+                deal_w2()
+                gaps = keep.tile([P, 512], F32, name="gaps_late", tag="w_raw", bufs=1)
+            gap = gaps[:, 256 * (t % 2) : 256 * (t % 2 + 1)]
+            gap_term(gap, lined, 256)
             for b in range(2):
                 add_turned(turned0[b][:, P * t : P * (t + 1)],
-                           [lined[:, 256 * b : 256 * (b + 1) : 2], lined[:, 256 * b + 1 : 256 * (b + 1) : 2], gap[:, P * b : P * (b + 1)]])
-        back0 = [turn_back(turned0[b], PACK) for b in range(2)]
-
-        w2_b = keep.tile([P, PACK * N], BF16, name="w2_b", align_bytes=64)
-        for c in range(2):
-            nc.scalar.copy(*deal_views(w2_b, w2_raw[c], c))
+                           [gap[:, P * b : P * (b + 1)], lined[:, 256 * b : 256 * (b + 1) : 2], lined[:, 256 * b + 1 : 256 * (b + 1) : 2]])
+        back0 = [turn_back(turned0[b], PACK, "staged0_%d" % b) for b in range(2)]
 
         lined1 = keep.tile([P, 1024], F32, name="lined1")
         for t in range(PACK):
             line_up(lined1[:, 256 * t : 256 * (t + 1)], t, 256, P)
-        gap1 = gap_term(lined1, 512)
+        gap1 = keep.tile([P, 512], F32, name="gap1", tag="staged0_0", bufs=1)
+        gap_term(gap1[:], lined1, 512)
         turned1 = psum.tile([P, BANK], F32, name="turned", tag="turned", bufs=3)
         for t in range(PACK):
             add_turned(turned1[:, P * t : P * (t + 1)],
-                       [lined1[:, 256 * t : 256 * (t + 1) : 2], lined1[:, 256 * t + 1 : 256 * (t + 1) : 2], gap1[:, P * t : P * (t + 1)]])
-        back1 = turn_back(turned1, PACK)
-
-        z0 = keep.tile([P, PACK * 256], BF16, name="z0", align_bytes=64)
-        for b in range(2):
-            gained(z0[:, 512 * b : 512 * (b + 1)], back0[b][:], gain)
-        w2_q = quantise(w2_b, 0, PACK * N, "w2q")
-        second_product(quantise(z0, 0, 1024, "z0q"), 0, 256)
+                       [gap1[:, P * t : P * (t + 1)], lined1[:, 256 * t : 256 * (t + 1) : 2], lined1[:, 256 * t + 1 : 256 * (t + 1) : 2]])
+        back1 = turn_back(turned1, PACK, "staged1")
 
         lined2 = keep.tile([P, 1024], F32, name="lined2")
         for t in range(PACK):
             line_up(lined2[:, 256 * t : 256 * (t + 1)], t, 384, P)
-        larger = keep.tile([P, 512], F32, name="larger")
-        nc.vector.tensor_tensor(larger[:], lined2[:, 0::2], lined2[:, 1::2], ALU.max)
+        z0 = keep.tile([P, PACK * 256], BF16, name="z0", tag="z0", bufs=1, align_bytes=64)
+        for b in range(2):
+            gained(z0[:, 512 * b : 512 * (b + 1)], back0[b][:], gain)
+        w2_q = quantise(w2_b, 0, PACK * N, "w2q")
+        z0_q = quantise(z0, 0, 1024, "z0q")
+        second_product(z0_q, 0, 256)
+
         smaller = keep.tile([P, 512], F32, name="smaller")
         nc.vector.tensor_tensor(smaller[:], lined2[:, 0::2], lined2[:, 1::2], ALU.min)
-        z1 = keep.tile([P, 512], BF16, name="z1", align_bytes=64)
-        gained(z1[:], back1[:], gain)
+        larger = keep.tile([P, 512], F32, name="larger", tag="z0", bufs=1, align_bytes=64)
+        nc.vector.tensor_tensor(larger[:], lined2[:, 0::2], lined2[:, 1::2], ALU.max)
+        z1 = keep.tile([P, 1024], BF16, name="z1", align_bytes=64)
         mixed = keep.tile([P, 512], F32, name="mixed")
         nc.vector.scalar_tensor_tensor(mixed[:], smaller[:], -0.5, larger[:], ALU.mult, ALU.add)
-        z1_q = quantise(z1, 0, 512, "z1q")
-        z2 = keep.tile([P, 512], BF16, name="z2", align_bytes=64)
-        gained(z2[:], mixed[:], gain4)
-        second_product(z1_q, 256, P)
-        second_product(quantise(z2, 0, 512, "z2q"), 384, P)
+        gained(z1[:, :512], back1[:], gain)
+        gained(z1[:, 512:], mixed[:], gain4)
+        second_product(quantise(z1, 0, 1024, "z1q"), 256, 256)
 
         out_rows = out.rearrange("(p t) v -> p t v", t=PACK)
-        W = 256
-        units = [(t, v0) for t in range(PACK) for v0 in range(0, V, W)]
+        units = [(t, v0, 256) for t in range(PACK) for v0 in (0, 256)][:-1]
+        tails = [(PACK - 1, 256, P), (PACK - 1, 384, P)]
 
-        def first_lookup(t, v0):
-            p1 = ring.tile([P, W], F32, name="p1", tag="p1")
-            nc.vector.tensor_scalar(p1[:], h[t][:].indirect(entries(n2_l, v0, W)), -1.0, 0.0, ALU.mult, ALU.add)
+        def fresh(name, n):
+            return keep.tile([P, n], F32, name=name, tag=name, bufs=9)
+
+        def first_lookup(t, v0, n):
+            p1 = fresh("p1", n)
+            nc.vector.tensor_scalar(p1[:], h[t][:].indirect(entries(n2_l, v0, n)), -1.0, 0.0, ALU.mult, ALU.add)
             return p1
 
-        p1_next = first_lookup(*units[0])
-        for u, (t, v0) in enumerate(units):
-            p1 = p1_next
-            e2 = ring.tile([P, W], F32, name="e2", tag="e2")
-            nc.vector.tensor_tensor(e2[:], h[t][:].indirect(entries(n3_l, v0, W)), p1[:], ALU.add)
-            lift = ring.tile([P, W], F32, name="lift", tag="lift")
+        def other_lookups(p1, t, v0, n):
+            e2 = fresh("e2", n)
+            nc.vector.tensor_tensor(e2[:], h[t][:].indirect(entries(n3_l, v0, n)), p1[:], ALU.add)
+            lift = fresh("lift", n)
             nc.scalar.activation(lift[:], e2[:], ACT.Relu, scale=-2.0)
-            e3 = ring.tile([P, W], F32, name="e3", tag="e3")
-            nc.vector.tensor_tensor(e3[:], h[t][:].indirect(entries(n4_l, v0, W)), p1[:], ALU.add)
-            if u + 1 < len(units):
-                p1_next = first_lookup(*units[u + 1])
-            over = ring.tile([P, W], F32, name="over", tag="over")
+            e3 = fresh("e3", n)
+            nc.vector.tensor_tensor(e3[:], h[t][:].indirect(entries(n4_l, v0, n)), p1[:], ALU.add)
+            return e2, e3, lift
+
+        def excess_term(e2, e3, n):
+            over = fresh("over", n)
             nc.vector.scalar_tensor_tensor(over[:], e2[:], 0.0, e3[:], ALU.min, ALU.subtract)
-            excess = ring.tile([P, W], F32, name="excess", tag="excess")
+            excess = fresh("excess", n)
             nc.scalar.activation(excess[:], over[:], ACT.Relu, scale=3.0)
-            second = ring.tile([P, W], F32, name="second", tag="second")
+            return excess
+
+        def second_term(e2, e3, n):
+            second = fresh("second", n)
             nc.vector.scalar_tensor_tensor(second[:], e2[:], 0.0, e3[:], ALU.max, ALU.min)
-            result = ring.tile([P, W], F32, name="result", tag="result")
-            if u + 1 < len(units):
-                turned = psum.tile([P, BANK], F32, name="turned", tag="turned", bufs=3)
-                for b in range(W // P):
-                    cols = slice(P * b, P * (b + 1))
-                    add_turned(turned[:, cols], [p1[:, cols], lift[:, cols], second[:, cols], excess[:, cols]])
-                back = turn_back(turned, W // P)
-                nc.scalar.copy(result[:], back[:, :W])
-            else:
-                part1 = keep.tile([P, W], F32, name="part1")
-                nc.vector.tensor_tensor(part1[:], p1[:], lift[:], ALU.add)
-                part2 = keep.tile([P, W], F32, name="part2")
-                nc.vector.tensor_tensor(part2[:], second[:], excess[:], ALU.add)
-                nc.vector.tensor_tensor(result[:], part1[:], part2[:], ALU.add)
-            nc.sync.dma_start(out_rows[:, t, v0 : v0 + W], result[:])
+            return second
+
+        def add(name, a, b, n):
+            total = fresh(name, n)
+            nc.vector.tensor_tensor(total[:], a[:], b[:], ALU.add)
+            return total
+
+        p1_next = first_lookup(*units[0])
+        for u, (t, v0, n) in enumerate(units):
+            p1 = p1_next
+            e2, e3, lift = other_lookups(p1, t, v0, n)
+            p1_next = first_lookup(*(units + tails)[u + 1])
+            excess = excess_term(e2, e3, n)
+            second = second_term(e2, e3, n)
+            turned = psum.tile([P, BANK], F32, name="turned", tag="turned", bufs=3)
+            for b in range(n // P):
+                cols = slice(P * b, P * (b + 1))
+                add_turned(turned[:, cols], [p1[:, cols], lift[:, cols], second[:, cols], excess[:, cols]])
+            back = turn_back(turned, n // P, "staged_u%d" % u)
+            result = fresh("result", n)
+            nc.scalar.copy(result[:], back[:, :n])
+            nc.sync.dma_start(out_rows[:, t, v0 : v0 + n], result[:])
+
+        def stt(name, in0, scalar, in1, op0, op1):
+            res = fresh(name, P)
+            nc.vector.scalar_tensor_tensor(res[:], in0[:], scalar, in1[:], op0, op1)
+            return res
+
+        def lookup_plus(name, lst, p1, t, v0, n):
+            e = fresh(name, n)
+            nc.vector.tensor_tensor(e[:], h[t][:].indirect(entries(lst, v0, n)), p1[:], ALU.add)
+            return e
+
+        pa = p1_next
+        ea2 = lookup_plus("e2", n3_l, pa, *tails[0])
+        ea3 = lookup_plus("e3", n4_l, pa, *tails[0])
+        pb = first_lookup(*tails[1])
+        over_a = stt("over", ea2, 0.0, ea3, ALU.min, ALU.subtract)
+        second_a = second_term(ea2, ea3, P)
+        base_a = stt("base", ea3, -2.0, pa, ALU.mult, ALU.add)
+        eb2 = lookup_plus("e2", n3_l, pb, *tails[1])
+        bent_a = stt("bent", over_a, -2.0, over_a, ALU.mult, ALU.max)
+        part_a = add("part", base_a, second_a, P)
+        eb3 = lookup_plus("e3", n4_l, pb, *tails[1])
+        result_a = add("result", part_a, bent_a, P)
+        nc.sync.dma_start(out_rows[:, PACK - 1, 256:384], result_a[:])
+        over_b = stt("over", eb2, 0.0, eb3, ALU.min, ALU.subtract)
+        second_b = second_term(eb2, eb3, P)
+        base_b = stt("base", eb3, -2.0, pb, ALU.mult, ALU.add)
+        bent_b = stt("bent", over_b, -2.0, over_b, ALU.mult, ALU.max)
+        part_b = add("part", base_b, second_b, P)
+        result_b = add("result", part_b, bent_b, P)
+        nc.sync.dma_start(out_rows[:, PACK - 1, 384:512], result_b[:])

@@ -38,8 +38,7 @@ def tile_picked_laypgaptop2_none_p_kernel(tc, x_words, x_scales, w1, gn, w2, off
         scale_tab = keep.tile([P, T], U8, name="scale_tab")
         nc.vector.memset(scale_tab[:].bitcast(I32), 0)
         offs_l = load_list(offs, "offs_l")
-        gain = keep.tile([P, PACK], F32, name="gain")
-        nc.sync.dma_start(gain[:], gn.rearrange("(p t) o -> p (t o)", t=PACK))
+        n1_l = load_list(n1, "n1_l")
         for q in range(4):
             nc.sync.dma_start(scale_tab[32 * q : 32 * q + 4, :].bitcast(I32), x_scales[0, 4 * q : 4 * q + 4, :].bitcast(I32))
         word_tab = keep.tile([P, T], I32, name="word_tab")
@@ -51,7 +50,8 @@ def tile_picked_laypgaptop2_none_p_kernel(tc, x_words, x_scales, w1, gn, w2, off
             return raw
 
         w1_raw = load_weight(w1)
-        n1_l = load_list(n1, "n1_l")
+        gain = keep.tile([P, PACK], F32, name="gain")
+        nc.sync.dma_start(gain[:], gn.rearrange("(p t) o -> p (t o)", t=PACK))
         n2_l = load_list(n2, "n2_l")
         n3_l = load_list(n3, "n3_l")
         n4_l = load_list(n4, "n4_l")
@@ -104,171 +104,143 @@ def tile_picked_laypgaptop2_none_p_kernel(tc, x_words, x_scales, w1, gn, w2, off
             for i, term in enumerate(terms):
                 nc.tensor.matmul(dst, term, ident[:], is_transpose=True, start=(i == 0), stop=(i == len(terms) - 1))
 
-        def turn_back(turned, blocks, tag):
-            staged = keep.tile([P, blocks * P], F32, name="staged", tag=tag, bufs=1)
-            nc.scalar.copy(staged[:], turned[:, : blocks * P])
-            back = psum.tile([P, BANK], F32, name="back", tag="back", bufs=2)
-            for b in range(blocks):
-                nc.tensor.transpose(back[:, P * b : P * (b + 1)], staged[:, P * b : P * (b + 1)], ident[:])
-            return back
+        def bank(i):
+            return psum.tile([P, BANK], F32, name="turned", tag="turned%d" % i, bufs=1)
+
+        def blocks(n):
+            return [slice(P * b, P * (b + 1)) for b in range(n // P)]
 
         def line_up(dst, t, v0, n):
             nc.vector.tensor_copy(dst, y[t][:].indirect(entries(n1_l, 2 * v0, 2 * n)))
 
-        def gap_term(gap, lined, n):
-            diff = keep.tile([P, n], F32, name="diff", tag="diff", bufs=5)
-            nc.vector.tensor_tensor(diff[:], lined[:, 0::2], lined[:, 1::2], ALU.subtract)
-            nc.scalar.activation(gap, diff[:], ACT.Abs, scale=3.0)
-
         def gained(z_b, src, g):
             nc.vector.tensor_tensor(z_b.rearrange("p (v t) -> p v t", t=PACK), src.rearrange("p (t v) -> p v t", t=PACK),
                                     g[:].unsqueeze(1).to_broadcast([P, P, PACK]), ALU.mult)
-
-        h = [keep.tile([P, V], F32, name="h%d" % t) for t in range(PACK)]
 
         def second_product(z_q, v0, n):
             for t in range(PACK):
                 acc = psum.tile([P, BANK], F32, name="acc", tag="mm", bufs=3)
                 nc.tensor.matmul_mx(out=acc[:, :n], lhsT=w2_q[0][:, P * t : P * (t + 1)].bitcast(FP8X4), lhsT_scale=w2_q[1][:, P * t : P * (t + 1)],
                                     rhs=z_q[0][:].bitcast(FP8X4), rhs_scale=z_q[1][:], start=True, stop=True)
-                nc.scalar.activation(h[t][:, v0 : v0 + n], acc[:, :n], ACT.Copy, scale=-0.5)
+                nc.scalar.activation(y[t][:, v0 : v0 + n], acc[:, :n], ACT.Copy, scale=-0.5)
 
         w2_b = keep.tile([P, PACK * N], BF16, name="w2_b", align_bytes=64)
-
-        def deal_w2():
-            for c in range(4):
-                nc.scalar.copy(w2_b[:].rearrange("p (t m j) -> p m t j", t=PACK, j=PACK)[:, 32 * c : 32 * (c + 1)],
-                               w2_raw[:].rearrange("p (j m t) -> p m t j", j=PACK, t=PACK)[:, 32 * c : 32 * (c + 1)])
-
-        turned0 = [psum.tile([P, BANK], F32, name="turned", tag="turned", bufs=3) for b in range(2)]
+        E = 384
+        turned = [bank(b) for b in range(E // P)]
         for t in range(PACK):
-            lined = keep.tile([P, 512], F32, name="lined0_%d" % t)
-            line_up(lined[:], t, 0, 256)
+            parts = [(0, 256), (256, P)]
+            lined = [keep.tile([P, 2 * n], F32, name="lined%d_%d" % (t, v0)) for v0, n in parts]
+            diff = [keep.tile([P, n], F32, name="diff", tag="diff%d_%d" % (t, v0), bufs=1) for v0, n in parts]
+            for i, (v0, n) in enumerate(parts):
+                line_up(lined[i][:], t, v0, n)
+            for i in range(2):
+                nc.vector.tensor_tensor(diff[i][:], lined[i][:, 0::2], lined[i][:, 1::2], ALU.subtract)
             if t == 0:
-                gaps = keep.tile([P, 512], F32, name="gaps_early")
+                gaps = keep.tile([P, 2 * E], F32, name="gaps_early")
             if t == 2:
-                deal_w2()
-                gaps = keep.tile([P, 512], F32, name="gaps_late", tag="w_raw", bufs=1)
-            gap = gaps[:, 256 * (t % 2) : 256 * (t % 2 + 1)]
-            gap_term(gap, lined, 256)
-            for b in range(2):
-                add_turned(turned0[b][:, P * t : P * (t + 1)],
-                           [gap[:, P * b : P * (b + 1)], lined[:, 256 * b : 256 * (b + 1) : 2], lined[:, 256 * b + 1 : 256 * (b + 1) : 2]])
-        back0 = [turn_back(turned0[b], PACK, "staged0_%d" % b) for b in range(2)]
+                for c in range(4):
+                    nc.scalar.copy(w2_b[:].rearrange("p (t m j) -> p m t j", t=PACK, j=PACK)[:, 32 * c : 32 * (c + 1)],
+                                   w2_raw[:].rearrange("p (j m t) -> p m t j", j=PACK, t=PACK)[:, 32 * c : 32 * (c + 1)])
+                gaps = keep.tile([P, 2 * E], F32, name="gaps_late", tag="w_raw", bufs=1)
+            gap = gaps[:, E * (t % 2) : E * (t % 2 + 1)]
+            for i, (v0, n) in enumerate(parts):
+                nc.scalar.activation(gap[:, v0 : v0 + n], diff[i][:], ACT.Abs, scale=3.0)
+            for b, cols in enumerate(blocks(E)):
+                both = lined[b // 2][:, 256 * (b % 2) : 256 * (b % 2 + 1)]
+                add_turned(turned[b][:, P * t : P * (t + 1)], [gap[:, cols], both[:, 0::2], both[:, 1::2]])
+        back = []
+        for b in range(E // P):
+            staged = keep.tile([P, BANK], F32, name="staged%d" % b)
+            nc.scalar.copy(staged[:], turned[b][:])
+            back.append(bank((3 + b) % 5))
+            for cols in blocks(BANK):
+                nc.tensor.transpose(back[b][:, cols], staged[:, cols], ident[:])
 
-        lined1 = keep.tile([P, 1024], F32, name="lined1")
+        lined = keep.tile([P, 1024], F32, name="lined_last", tag="diff0_256", bufs=1)
         for t in range(PACK):
-            line_up(lined1[:, 256 * t : 256 * (t + 1)], t, 256, P)
-        gap1 = keep.tile([P, 512], F32, name="gap1", tag="staged0_0", bufs=1)
-        gap_term(gap1[:], lined1, 512)
-        turned1 = psum.tile([P, BANK], F32, name="turned", tag="turned", bufs=3)
-        for t in range(PACK):
-            add_turned(turned1[:, P * t : P * (t + 1)],
-                       [gap1[:, P * t : P * (t + 1)], lined1[:, 256 * t : 256 * (t + 1) : 2], lined1[:, 256 * t + 1 : 256 * (t + 1) : 2]])
-        back1 = turn_back(turned1, PACK, "staged1")
-
-        lined2 = keep.tile([P, 1024], F32, name="lined2")
-        for t in range(PACK):
-            line_up(lined2[:, 256 * t : 256 * (t + 1)], t, 384, P)
-        z0 = keep.tile([P, PACK * 256], BF16, name="z0", tag="z0", bufs=1, align_bytes=64)
-        for b in range(2):
-            gained(z0[:, 512 * b : 512 * (b + 1)], back0[b][:], gain)
+            line_up(lined[:, 256 * t : 256 * (t + 1)], t, E, P)
         w2_q = quantise(w2_b, 0, PACK * N, "w2q")
-        z0_q = quantise(z0, 0, 1024, "z0q")
-        second_product(z0_q, 0, 256)
-
         smaller = keep.tile([P, 512], F32, name="smaller")
-        nc.vector.tensor_tensor(smaller[:], lined2[:, 0::2], lined2[:, 1::2], ALU.min)
-        larger = keep.tile([P, 512], F32, name="larger", tag="z0", bufs=1, align_bytes=64)
-        nc.vector.tensor_tensor(larger[:], lined2[:, 0::2], lined2[:, 1::2], ALU.max)
-        z1 = keep.tile([P, 1024], BF16, name="z1", align_bytes=64)
-        mixed = keep.tile([P, 512], F32, name="mixed")
+        nc.vector.tensor_tensor(smaller[:], lined[:, 0::2], lined[:, 1::2], ALU.min)
+        larger = keep.tile([P, 512], F32, name="larger")
+        nc.vector.tensor_tensor(larger[:], lined[:, 0::2], lined[:, 1::2], ALU.max)
+        z01 = keep.tile([P, 1024], BF16, name="z01", tag="z01", bufs=1, align_bytes=64)
+        for b in range(2):
+            gained(z01[:, 512 * b : 512 * (b + 1)], back[b][:], gain)
+        z2 = keep.tile([P, 512], BF16, name="z2", align_bytes=64)
+        gained(z2[:], back[2][:], gain)
+        second_product(quantise(z01, 0, 1024, "z01q"), 0, 256)
+        mixed = keep.tile([P, 512], F32, name="mixed", tag="z01", bufs=1, align_bytes=64)
         nc.vector.scalar_tensor_tensor(mixed[:], smaller[:], -0.5, larger[:], ALU.mult, ALU.add)
-        gained(z1[:, :512], back1[:], gain)
-        gained(z1[:, 512:], mixed[:], gain4)
-        second_product(quantise(z1, 0, 1024, "z1q"), 256, 256)
+        second_product(quantise(z2, 0, 512, "z2q"), 256, P)
+        z3 = keep.tile([P, 512], BF16, name="z3", align_bytes=64)
+        gained(z3[:], mixed[:], gain4)
+        second_product(quantise(z3, 0, 512, "z3q"), E, P)
 
         out_rows = out.rearrange("(p t) v -> p t v", t=PACK)
-        units = [(t, v0, 256) for t in range(PACK) for v0 in (0, 256)][:-1]
-        tails = [(PACK - 1, 256, P), (PACK - 1, 384, P)]
+        units = [(t, v0, 256) for t in range(PACK) for v0 in (0, 256)]
 
-        def fresh(name, n):
-            return keep.tile([P, n], F32, name=name, tag=name, bufs=9)
+        def fresh(name, n, tag=None):
+            if tag is None:
+                return keep.tile([P, n], F32, name=name, tag=name, bufs=len(units))
+            return keep.tile([P, n], F32, name=name, tag=tag, bufs=1)
 
         def first_lookup(t, v0, n):
             p1 = fresh("p1", n)
-            nc.vector.tensor_scalar(p1[:], h[t][:].indirect(entries(n2_l, v0, n)), -1.0, 0.0, ALU.mult, ALU.add)
+            nc.vector.tensor_scalar(p1[:], y[t][:].indirect(entries(n2_l, v0, n)), -1.0, 0.0, ALU.mult, ALU.add)
             return p1
 
-        def other_lookups(p1, t, v0, n):
-            e2 = fresh("e2", n)
-            nc.vector.tensor_tensor(e2[:], h[t][:].indirect(entries(n3_l, v0, n)), p1[:], ALU.add)
-            lift = fresh("lift", n)
-            nc.scalar.activation(lift[:], e2[:], ACT.Relu, scale=-2.0)
-            e3 = fresh("e3", n)
-            nc.vector.tensor_tensor(e3[:], h[t][:].indirect(entries(n4_l, v0, n)), p1[:], ALU.add)
-            return e2, e3, lift
+        def lookup_plus(name, lst, p1, t, v0, n, tag=None):
+            e = fresh(name, n, tag)
+            nc.vector.tensor_tensor(e[:], y[t][:].indirect(entries(lst, v0, n)), p1[:], ALU.add)
+            return e
 
-        def excess_term(e2, e3, n):
-            over = fresh("over", n)
-            nc.vector.scalar_tensor_tensor(over[:], e2[:], 0.0, e3[:], ALU.min, ALU.subtract)
-            excess = fresh("excess", n)
-            nc.scalar.activation(excess[:], over[:], ACT.Relu, scale=3.0)
-            return excess
+        def relu(name, src, scale, n, tag):
+            res = fresh(name, n, tag)
+            nc.scalar.activation(res[:], src, ACT.Relu, scale=scale)
+            return res
 
-        def second_term(e2, e3, n):
-            second = fresh("second", n)
-            nc.vector.scalar_tensor_tensor(second[:], e2[:], 0.0, e3[:], ALU.max, ALU.min)
-            return second
+        def stt(name, in0, in1, op0, op1, n, tag=None):
+            res = fresh(name, n, tag)
+            nc.vector.scalar_tensor_tensor(res[:], in0[:], 0.0, in1[:], op0, op1)
+            return res
 
         def add(name, a, b, n):
             total = fresh(name, n)
             nc.vector.tensor_tensor(total[:], a[:], b[:], ALU.add)
             return total
 
+        def turned_sum(terms, n, i):
+            acc = bank(i)
+            for cols in blocks(n):
+                add_turned(acc[:, cols], [term[:, cols] for term in terms])
+            return acc
+
+        def evicted(name, acc, n):
+            res = fresh(name, n)
+            nc.scalar.copy(res[:], acc[:, :n])
+            return res
+
         p1_next = first_lookup(*units[0])
         for u, (t, v0, n) in enumerate(units):
             p1 = p1_next
-            e2, e3, lift = other_lookups(p1, t, v0, n)
-            p1_next = first_lookup(*(units + tails)[u + 1])
-            excess = excess_term(e2, e3, n)
-            second = second_term(e2, e3, n)
-            turned = psum.tile([P, BANK], F32, name="turned", tag="turned", bufs=3)
-            for b in range(n // P):
-                cols = slice(P * b, P * (b + 1))
-                add_turned(turned[:, cols], [p1[:, cols], lift[:, cols], second[:, cols], excess[:, cols]])
-            back = turn_back(turned, n // P, "staged_u%d" % u)
-            result = fresh("result", n)
-            nc.scalar.copy(result[:], back[:, :n])
+            e2 = lookup_plus("e2", n3_l, p1, t, v0, n)
+            e3 = lookup_plus("e3", n4_l, p1, t, v0, n)
+            if u + 1 < len(units):
+                p1_next = first_lookup(*units[u + 1])
+            if u + 1 < len(units):
+                lift = relu("lift", e2[:], -2.0, n, "lift%d" % (u % 2))
+                over = stt("over", e2, e3, ALU.min, ALU.subtract, n)
+                excess = relu("excess", over[:], 3.0, n, "excess")
+                second = stt("second", e2, e3, ALU.max, ALU.min, n, "second%d" % u)
+                staged = evicted("staged", turned_sum([p1, lift, second, excess], n, u % 2), n)
+                result = evicted("result", turned_sum([staged], n, 2 + u % 2), n)
+            else:
+                lift = relu("lift", e2[:], -2.0, n, "second%d" % (u - 2))
+                base = add("base", p1, lift, n)
+                over = stt("over", e2, e3, ALU.min, ALU.subtract, n)
+                second = stt("second", e2, e3, ALU.max, ALU.min, n)
+                excess = fresh("last_excess", n)
+                nc.vector.tensor_scalar(excess[:], over[:], 3.0, 0.0, ALU.mult, ALU.max)
+                result = add("result", add("part", base, second, n), excess, n)
             nc.sync.dma_start(out_rows[:, t, v0 : v0 + n], result[:])
-
-        def stt(name, in0, scalar, in1, op0, op1):
-            res = fresh(name, P)
-            nc.vector.scalar_tensor_tensor(res[:], in0[:], scalar, in1[:], op0, op1)
-            return res
-
-        def lookup_plus(name, lst, p1, t, v0, n):
-            e = fresh(name, n)
-            nc.vector.tensor_tensor(e[:], h[t][:].indirect(entries(lst, v0, n)), p1[:], ALU.add)
-            return e
-
-        pa = p1_next
-        ea2 = lookup_plus("e2", n3_l, pa, *tails[0])
-        ea3 = lookup_plus("e3", n4_l, pa, *tails[0])
-        pb = first_lookup(*tails[1])
-        over_a = stt("over", ea2, 0.0, ea3, ALU.min, ALU.subtract)
-        second_a = second_term(ea2, ea3, P)
-        base_a = stt("base", ea3, -2.0, pa, ALU.mult, ALU.add)
-        eb2 = lookup_plus("e2", n3_l, pb, *tails[1])
-        bent_a = stt("bent", over_a, -2.0, over_a, ALU.mult, ALU.max)
-        part_a = add("part", base_a, second_a, P)
-        eb3 = lookup_plus("e3", n4_l, pb, *tails[1])
-        result_a = add("result", part_a, bent_a, P)
-        nc.sync.dma_start(out_rows[:, PACK - 1, 256:384], result_a[:])
-        over_b = stt("over", eb2, 0.0, eb3, ALU.min, ALU.subtract)
-        second_b = second_term(eb2, eb3, P)
-        base_b = stt("base", eb3, -2.0, pb, ALU.mult, ALU.add)
-        bent_b = stt("bent", over_b, -2.0, over_b, ALU.mult, ALU.max)
-        part_b = add("part", base_b, second_b, P)
-        result_b = add("result", part_b, bent_b, P)
-        nc.sync.dma_start(out_rows[:, PACK - 1, 384:512], result_b[:])

@@ -19,6 +19,8 @@ ACT = mybir.ActivationFunctionType
 P = 128
 PACK = 4
 BANK = 512
+HALF = 256
+EARLY = 384
 
 
 def tile_picked_laypgaptop2_none_p_kernel(tc, x_words, x_scales, w1, gn, w2, offs, n1, n2, n3, n4, out):
@@ -32,8 +34,37 @@ def tile_picked_laypgaptop2_none_p_kernel(tc, x_words, x_scales, w1, gn, w2, off
             nc.sync.dma_start(lst[:], src)
             return lst
 
+        def load_weight(w):
+            raw = keep.tile([P, PACK * w.shape[1]], F32, name="w_raw", tag="w_raw")
+            nc.sync.dma_start(raw[:], w.rearrange("(p j) c -> p (j c)", j=PACK))
+            return raw
+
         def entries(lst, first, count):
             return lst[:, first // 16 : (first + count) // 16]
+
+        def quantise(grouped, name):
+            width = grouped.shape[1] // PACK
+            codes = keep.tile([P, width], U32, name=name + "_code", align_bytes=64)
+            scales = keep.tile([P, width], U8, name=name + "_scale", align_bytes=64)
+            nc.vector.quantize_mx(out=codes[:].bitcast(FP8X4), scales=scales[:], in_=grouped[:])
+            return codes, scales
+
+        def product(dst, lhs_codes, lhs_scales, rhs_codes, rhs_scales, factor):
+            width = dst.shape[1]
+            acc = psum.tile([P, BANK], F32, name="acc", tag="acc", bufs=3)
+            nc.tensor.matmul_mx(out=acc[:, :width], lhsT=lhs_codes.bitcast(FP8X4), lhsT_scale=lhs_scales,
+                                rhs=rhs_codes.bitcast(FP8X4), rhs_scale=rhs_scales, start=True, stop=True)
+            nc.scalar.activation(dst, acc[:, :width], ACT.Copy, scale=factor)
+
+        def bank(i):
+            return psum.tile([P, BANK], F32, name="sums", tag="sums%d" % i)
+
+        def blocks(width):
+            return [slice(c, c + P) for c in range(0, width, P)]
+
+        def add_turned(dst, terms):
+            for i, term in enumerate(terms):
+                nc.tensor.matmul(dst, term, ident[:], is_transpose=True, start=(i == 0), stop=(i == len(terms) - 1))
 
         scale_tab = keep.tile([P, T], U8, name="scale_tab")
         nc.vector.memset(scale_tab[:].bitcast(I32), 0)
@@ -43,12 +74,6 @@ def tile_picked_laypgaptop2_none_p_kernel(tc, x_words, x_scales, w1, gn, w2, off
             nc.sync.dma_start(scale_tab[32 * q : 32 * q + 4, :].bitcast(I32), x_scales[0, 4 * q : 4 * q + 4, :].bitcast(I32))
         word_tab = keep.tile([P, T], I32, name="word_tab")
         nc.sync.dma_start(word_tab[:], x_words[0].rearrange("p n t -> p (n t)").bitcast(I32))
-
-        def load_weight(w):
-            raw = keep.tile([P, PACK * 512], F32, name="w_raw", tag="w_raw", bufs=1)
-            nc.sync.dma_start(raw[:], w.rearrange("(p j) c -> p (j c)", j=PACK))
-            return raw
-
         w1_raw = load_weight(w1)
         gain = keep.tile([P, PACK], F32, name="gain")
         nc.sync.dma_start(gain[:], gn.rearrange("(p t) o -> p (t o)", t=PACK))
@@ -64,183 +89,154 @@ def tile_picked_laypgaptop2_none_p_kernel(tc, x_words, x_scales, w1, gn, w2, off
         x_scale = keep.tile([P, S], U8, name="x_scale", align_bytes=64)
         nc.vector.tensor_copy(x_scale[:], scale_tab[:].indirect(offs_l[:]))
         x_code = []
-        for c in range(2):
+        for c in range(S // BANK):
             codes = keep.tile([P, BANK], U32, name="x_code%d" % c, align_bytes=64)
             nc.vector.tensor_copy(codes[:], word_tab[:].bitcast(U32).indirect(entries(offs_l, BANK * c, BANK)))
             x_code.append(codes)
 
-        def quantise(grouped, first, width, name):
-            codes = keep.tile([P, width // PACK], U32, name=name + "_code", align_bytes=64)
-            scales = keep.tile([P, width // PACK], U8, name=name + "_scale", align_bytes=64)
-            nc.vector.quantize_mx(out=codes[:].bitcast(FP8X4), scales=scales[:], in_=grouped[:, first : first + width])
-            return codes, scales
-
-        w1_b = [keep.tile([P, 512], BF16, name="w1_b%d" % t, align_bytes=64) for t in range(PACK)]
+        w1_b = [keep.tile([P, PACK * P], BF16, name="w1_b%d" % t, align_bytes=64) for t in range(PACK)]
         w1_cols = w1_raw[:].rearrange("p (j m t) -> p t m j", j=PACK, t=PACK)
 
         def deal_w1(copy, t):
             copy(w1_b[t][:].rearrange("p (m j) -> p m j", j=PACK), w1_cols[:, t])
 
-        w1_q = [None] * PACK
         deal_w1(nc.vector.tensor_copy, 0)
         deal_w1(nc.scalar.copy, 1)
-        w1_q[0] = quantise(w1_b[0], 0, 512, "w1q0")
-        deal_w1(nc.vector.tensor_copy, 2)
-        w1_q[1] = quantise(w1_b[1], 0, 512, "w1q1")
-        deal_w1(nc.vector.tensor_copy, 3)
-        w1_q[2] = quantise(w1_b[2], 0, 512, "w1q2")
-        w1_q[3] = quantise(w1_b[3], 0, 512, "w1q3")
+        w1_q = [quantise(w1_b[0], "w1q0")]
+        for t in range(2, PACK):
+            deal_w1(nc.vector.tensor_copy, t)
+            w1_q.append(quantise(w1_b[t - 1], "w1q%d" % (t - 1)))
+        w1_q.append(quantise(w1_b[PACK - 1], "w1q%d" % (PACK - 1)))
         w2_raw = load_weight(w2)
 
-        y = [keep.tile([P, S], F32, name="y%d" % t) for t in range(PACK)]
+        rows = [keep.tile([P, S], F32, name="rows%d" % t) for t in range(PACK)]
         for t in range(PACK):
-            for c in range(2):
-                acc = psum.tile([P, BANK], F32, name="acc", tag="mm", bufs=3)
-                nc.tensor.matmul_mx(out=acc[:], lhsT=w1_q[t][0][:].bitcast(FP8X4), lhsT_scale=w1_q[t][1][:],
-                                    rhs=x_code[c][:].bitcast(FP8X4), rhs_scale=x_scale[:, BANK * c : BANK * (c + 1)], start=True, stop=True)
-                nc.scalar.activation(y[t][:, BANK * c : BANK * (c + 1)], acc[:], ACT.Copy, scale=0.25)
+            for c in range(S // BANK):
+                cols = slice(BANK * c, BANK * (c + 1))
+                product(rows[t][:, cols], w1_q[t][0][:], w1_q[t][1][:], x_code[c][:], x_scale[:, cols], 0.25)
 
-        def add_turned(dst, terms):
-            for i, term in enumerate(terms):
-                nc.tensor.matmul(dst, term, ident[:], is_transpose=True, start=(i == 0), stop=(i == len(terms) - 1))
+        def line_up(dst, t, v0, count):
+            nc.vector.tensor_copy(dst, rows[t][:].indirect(entries(n1_l, 2 * v0, 2 * count)))
 
-        def bank(i):
-            return psum.tile([P, BANK], F32, name="turned", tag="turned%d" % i, bufs=1)
+        def gained(dst, src, factors):
+            nc.vector.tensor_tensor(dst.rearrange("p (v t) -> p v t", t=PACK), src.rearrange("p (t v) -> p v t", t=PACK),
+                                    factors[:].unsqueeze(1).to_broadcast([P, P, PACK]), ALU.mult)
 
-        def blocks(n):
-            return [slice(P * b, P * (b + 1)) for b in range(n // P)]
-
-        def line_up(dst, t, v0, n):
-            nc.vector.tensor_copy(dst, y[t][:].indirect(entries(n1_l, 2 * v0, 2 * n)))
-
-        def gained(z_b, src, g):
-            nc.vector.tensor_tensor(z_b.rearrange("p (v t) -> p v t", t=PACK), src.rearrange("p (t v) -> p v t", t=PACK),
-                                    g[:].unsqueeze(1).to_broadcast([P, P, PACK]), ALU.mult)
-
-        def second_product(z_q, v0, n):
-            for t in range(PACK):
-                acc = psum.tile([P, BANK], F32, name="acc", tag="mm", bufs=3)
-                nc.tensor.matmul_mx(out=acc[:, :n], lhsT=w2_q[0][:, P * t : P * (t + 1)].bitcast(FP8X4), lhsT_scale=w2_q[1][:, P * t : P * (t + 1)],
-                                    rhs=z_q[0][:].bitcast(FP8X4), rhs_scale=z_q[1][:], start=True, stop=True)
-                nc.scalar.activation(y[t][:, v0 : v0 + n], acc[:, :n], ACT.Copy, scale=-0.5)
+        def second_product(z_q, v0, count):
+            for t, cols in enumerate(blocks(N)):
+                product(rows[t][:, v0 : v0 + count], w2_q[0][:, cols], w2_q[1][:, cols], z_q[0][:], z_q[1][:], -0.5)
 
         w2_b = keep.tile([P, PACK * N], BF16, name="w2_b", align_bytes=64)
-        E = 384
-        turned = [bank(b) for b in range(E // P)]
+        parts = [(0, 2 * P), (2 * P, P)]
+        turned = [bank(b) for b in range(EARLY // P)]
         for t in range(PACK):
-            parts = [(0, 256), (256, P)]
-            lined = [keep.tile([P, 2 * n], F32, name="lined%d_%d" % (t, v0)) for v0, n in parts]
-            diff = [keep.tile([P, n], F32, name="diff", tag="diff%d_%d" % (t, v0), bufs=1) for v0, n in parts]
-            for i, (v0, n) in enumerate(parts):
-                line_up(lined[i][:], t, v0, n)
-            for i in range(2):
+            lined = [keep.tile([P, 2 * count], F32, name="lined%d_%d" % (t, v0)) for v0, count in parts]
+            diff = [keep.tile([P, count], F32, name="diff", tag="diff%d_%d" % (t, v0)) for v0, count in parts]
+            for i, (v0, count) in enumerate(parts):
+                line_up(lined[i][:], t, v0, count)
+            for i in range(len(parts)):
                 nc.vector.tensor_tensor(diff[i][:], lined[i][:, 0::2], lined[i][:, 1::2], ALU.subtract)
             if t == 0:
-                gaps = keep.tile([P, 2 * E], F32, name="gaps_early")
+                gaps = keep.tile([P, 2 * EARLY], F32, name="gaps_early")
             if t == 2:
                 for c in range(4):
                     nc.scalar.copy(w2_b[:].rearrange("p (t m j) -> p m t j", t=PACK, j=PACK)[:, 32 * c : 32 * (c + 1)],
                                    w2_raw[:].rearrange("p (j m t) -> p m t j", j=PACK, t=PACK)[:, 32 * c : 32 * (c + 1)])
-                gaps = keep.tile([P, 2 * E], F32, name="gaps_late", tag="w_raw", bufs=1)
-            gap = gaps[:, E * (t % 2) : E * (t % 2 + 1)]
-            for i, (v0, n) in enumerate(parts):
-                nc.scalar.activation(gap[:, v0 : v0 + n], diff[i][:], ACT.Abs, scale=3.0)
-            for b, cols in enumerate(blocks(E)):
-                both = lined[b // 2][:, 256 * (b % 2) : 256 * (b % 2 + 1)]
+                gaps = keep.tile([P, 2 * EARLY], F32, name="gaps_late", tag="w_raw")
+            gap = gaps[:, EARLY * (t % 2) : EARLY * (t % 2 + 1)]
+            for i, (v0, count) in enumerate(parts):
+                nc.scalar.activation(gap[:, v0 : v0 + count], diff[i][:], ACT.Abs, scale=3.0)
+            for b, cols in enumerate(blocks(EARLY)):
+                both = lined[b // 2][:, 2 * P * (b % 2) : 2 * P * (b % 2 + 1)]
                 add_turned(turned[b][:, P * t : P * (t + 1)], [gap[:, cols], both[:, 0::2], both[:, 1::2]])
         back = []
-        for b in range(E // P):
+        for b in range(EARLY // P):
             staged = keep.tile([P, BANK], F32, name="staged%d" % b)
             nc.scalar.copy(staged[:], turned[b][:])
-            back.append(bank((3 + b) % 5))
+            back.append(bank((len(turned) + b) % 5))
             for cols in blocks(BANK):
                 nc.tensor.transpose(back[b][:, cols], staged[:, cols], ident[:])
 
-        lined = keep.tile([P, 1024], F32, name="lined_last", tag="diff0_256", bufs=1)
+        lined_late = keep.tile([P, 2 * P * PACK], F32, name="lined_late", tag="diff0_%d" % parts[1][0])
         for t in range(PACK):
-            line_up(lined[:, 256 * t : 256 * (t + 1)], t, E, P)
-        w2_q = quantise(w2_b, 0, PACK * N, "w2q")
-        smaller = keep.tile([P, 512], F32, name="smaller")
-        nc.vector.tensor_tensor(smaller[:], lined[:, 0::2], lined[:, 1::2], ALU.min)
-        larger = keep.tile([P, 512], F32, name="larger")
-        nc.vector.tensor_tensor(larger[:], lined[:, 0::2], lined[:, 1::2], ALU.max)
-        z01 = keep.tile([P, 1024], BF16, name="z01", tag="z01", bufs=1, align_bytes=64)
+            line_up(lined_late[:, 2 * P * t : 2 * P * (t + 1)], t, EARLY, P)
+        w2_q = quantise(w2_b, "w2q")
+        smaller = keep.tile([P, PACK * P], F32, name="smaller")
+        nc.vector.tensor_tensor(smaller[:], lined_late[:, 0::2], lined_late[:, 1::2], ALU.min)
+        larger = keep.tile([P, PACK * P], F32, name="larger")
+        nc.vector.tensor_tensor(larger[:], lined_late[:, 0::2], lined_late[:, 1::2], ALU.max)
+        z01 = keep.tile([P, 2 * BANK], BF16, name="z01", tag="z01", align_bytes=64)
         for b in range(2):
-            gained(z01[:, 512 * b : 512 * (b + 1)], back[b][:], gain)
-        z2 = keep.tile([P, 512], BF16, name="z2", align_bytes=64)
+            gained(z01[:, BANK * b : BANK * (b + 1)], back[b][:], gain)
+        z2 = keep.tile([P, BANK], BF16, name="z2", align_bytes=64)
         gained(z2[:], back[2][:], gain)
-        second_product(quantise(z01, 0, 1024, "z01q"), 0, 256)
-        mixed = keep.tile([P, 512], F32, name="mixed", tag="z01", bufs=1, align_bytes=64)
+        second_product(quantise(z01, "z01q"), 0, 2 * P)
+        mixed = keep.tile([P, PACK * P], F32, name="mixed", tag="z01", align_bytes=64)
         nc.vector.scalar_tensor_tensor(mixed[:], smaller[:], -0.5, larger[:], ALU.mult, ALU.add)
-        second_product(quantise(z2, 0, 512, "z2q"), 256, P)
-        z3 = keep.tile([P, 512], BF16, name="z3", align_bytes=64)
+        second_product(quantise(z2, "z2q"), 2 * P, P)
+        z3 = keep.tile([P, BANK], BF16, name="z3", align_bytes=64)
         gained(z3[:], mixed[:], gain4)
-        second_product(quantise(z3, 0, 512, "z3q"), E, P)
+        second_product(quantise(z3, "z3q"), EARLY, P)
 
         out_rows = out.rearrange("(p t) v -> p t v", t=PACK)
-        units = [(t, v0, 256) for t in range(PACK) for v0 in (0, 256)]
+        units = [(t, v0, HALF) for t in range(PACK - 1) for v0 in range(0, V, HALF)] + [(PACK - 1, 0, V)]
 
-        def fresh(name, n, tag=None):
-            if tag is None:
-                return keep.tile([P, n], F32, name=name, tag=name, bufs=len(units))
-            return keep.tile([P, n], F32, name=name, tag=tag, bufs=1)
+        def fresh(name, width):
+            return keep.tile([P, width], F32, name=name, tag=name, bufs=len(units))
 
-        def first_lookup(t, v0, n):
-            p1 = fresh("p1", n)
-            nc.vector.tensor_scalar(p1[:], y[t][:].indirect(entries(n2_l, v0, n)), -1.0, 0.0, ALU.mult, ALU.add)
+        def first_lookup(t, v0, count):
+            p1 = fresh("p1", count)
+            nc.vector.tensor_scalar(p1[:], rows[t][:].indirect(entries(n2_l, v0, count)), -1.0, 0.0, ALU.mult, ALU.add)
             return p1
 
-        def lookup_plus(name, lst, p1, t, v0, n, tag=None):
-            e = fresh(name, n, tag)
-            nc.vector.tensor_tensor(e[:], y[t][:].indirect(entries(lst, v0, n)), p1[:], ALU.add)
-            return e
-
-        def relu(name, src, scale, n, tag):
-            res = fresh(name, n, tag)
-            nc.scalar.activation(res[:], src, ACT.Relu, scale=scale)
-            return res
-
-        def stt(name, in0, in1, op0, op1, n, tag=None):
-            res = fresh(name, n, tag)
-            nc.vector.scalar_tensor_tensor(res[:], in0[:], 0.0, in1[:], op0, op1)
-            return res
-
-        def add(name, a, b, n):
-            total = fresh(name, n)
-            nc.vector.tensor_tensor(total[:], a[:], b[:], ALU.add)
+        def lookup_plus(name, lst, p1, t, v0, count):
+            total = fresh(name, count)
+            nc.vector.tensor_tensor(total[:], rows[t][:].indirect(entries(lst, v0, count)), p1[:], ALU.add)
             return total
 
-        def turned_sum(terms, n, i):
-            acc = bank(i)
-            for cols in blocks(n):
-                add_turned(acc[:, cols], [term[:, cols] for term in terms])
-            return acc
-
-        def evicted(name, acc, n):
-            res = fresh(name, n)
-            nc.scalar.copy(res[:], acc[:, :n])
+        def combine(name, in0, scalar, in1, op0, op1):
+            res = fresh(name, in0.shape[1])
+            nc.vector.scalar_tensor_tensor(res[:], in0[:], scalar, in1[:], op0, op1)
             return res
 
+        def turned_sum(terms, i):
+            acc = bank(i)
+            for cols in blocks(HALF):
+                add_turned(acc[:, cols], [term[:, cols] for term in terms])
+            return acc[:, :HALF]
+
         p1_next = first_lookup(*units[0])
-        for u, (t, v0, n) in enumerate(units):
+        for u, (t, v0, count) in enumerate(units[:-1]):
             p1 = p1_next
-            e2 = lookup_plus("e2", n3_l, p1, t, v0, n)
-            e3 = lookup_plus("e3", n4_l, p1, t, v0, n)
-            if u + 1 < len(units):
-                p1_next = first_lookup(*units[u + 1])
-            if u + 1 < len(units):
-                lift = relu("lift", e2[:], -2.0, n, "lift%d" % (u % 2))
-                over = stt("over", e2, e3, ALU.min, ALU.subtract, n)
-                excess = relu("excess", over[:], 3.0, n, "excess")
-                second = stt("second", e2, e3, ALU.max, ALU.min, n, "second%d" % u)
-                staged = evicted("staged", turned_sum([p1, lift, second, excess], n, u % 2), n)
-                result = evicted("result", turned_sum([staged], n, 2 + u % 2), n)
-            else:
-                lift = relu("lift", e2[:], -2.0, n, "second%d" % (u - 2))
-                base = add("base", p1, lift, n)
-                over = stt("over", e2, e3, ALU.min, ALU.subtract, n)
-                second = stt("second", e2, e3, ALU.max, ALU.min, n)
-                excess = fresh("last_excess", n)
-                nc.vector.tensor_scalar(excess[:], over[:], 3.0, 0.0, ALU.mult, ALU.max)
-                result = add("result", add("part", base, second, n), excess, n)
-            nc.sync.dma_start(out_rows[:, t, v0 : v0 + n], result[:])
+            e2 = lookup_plus("e2", n3_l, p1, t, v0, count)
+            e3 = lookup_plus("e3", n4_l, p1, t, v0, count)
+            p1_next = first_lookup(*units[u + 1])
+            half = keep.tile([P, HALF], F32, name="half", tag="half")
+            nc.scalar.activation(half[:], e2[:], ACT.Relu, scale=-1.0)
+            lift = keep.tile([P, HALF], F32, name="lift", tag="lift")
+            nc.scalar.activation(lift[:], e2[:], ACT.Relu, scale=-2.0)
+            capped = combine("capped", e2, 0.0, e3, ALU.max, ALU.min)
+            excess = fresh("excess", HALF)
+            nc.scalar.activation(excess[:], turned_sum([half, e3], 0), ACT.Relu, scale=-3.0)
+            rest = fresh("rest", HALF)
+            nc.scalar.copy(rest[:], turned_sum([lift, p1, capped], 1))
+            result = fresh("result", HALF)
+            nc.scalar.copy(result[:], turned_sum([excess, rest], 2 + u % 2))
+            nc.sync.dma_start(out_rows[:, t, v0 : v0 + HALF], result[:])
+
+        t, v0, count = units[-1]
+        p1 = p1_next
+        e2 = lookup_plus("e2", n3_l, p1, t, v0, count)
+        e3 = lookup_plus("e3", n4_l, p1, t, v0, count)
+        over = combine("over", e2, 0.0, e3, ALU.min, ALU.subtract)
+        base = combine("base", e3, -2.0, p1, ALU.mult, ALU.add)
+        capped = combine("capped", e2, 0.0, e3, ALU.max, ALU.min)
+        bent = combine("bent", over, -2.0, over, ALU.mult, ALU.max)
+        halves = [slice(c, c + HALF) for c in range(0, V, HALF)]
+        partial = [fresh("partial", HALF) for cols in halves]
+        for i, cols in enumerate(halves):
+            nc.vector.tensor_tensor(partial[i][:], base[:, cols], capped[:, cols], ALU.add)
+        for i, cols in enumerate(halves):
+            result = fresh("last_result", HALF)
+            nc.vector.tensor_tensor(result[:], partial[i][:], bent[:, cols], ALU.add)
+            nc.sync.dma_start(out_rows[:, t, cols], result[:])

from contextlib import ExitStack

import concourse.mybir as mybir
from concourse.masks import make_identity

K, T, S, V, H, N = 512, 2048, 1024, 512, 512, 512
FLOPS = 2 * K * H * S + 2 * H * N * V

F32 = mybir.dt.float32
BF16 = mybir.dt.bfloat16
I32 = mybir.dt.int32
U32 = mybir.dt.uint32
U16 = mybir.dt.uint16
U8 = mybir.dt.uint8
FP8X4 = mybir.dt.float8_e4m3fn_x4
ALU = mybir.AluOpType
ACT = mybir.ActivationFunctionType

P = 128
PACK = 4
BANK = 512
HALF = 256
EARLY = 384


def tile_picked_laypgaptop2_none_p_kernel(tc, x_words, x_scales, w1, gn, w2, offs, n1, n2, n3, n4, out):
    nc = tc.nc
    with ExitStack() as ctx:
        keep = ctx.enter_context(tc.tile_pool(name="keep", bufs=1))
        psum = ctx.enter_context(tc.psum_pool(name="psum", bufs=1))

        def load_list(src, name):
            lst = keep.tile(list(src.shape), U16, name=name)
            nc.sync.dma_start(lst[:], src)
            return lst

        def load_weight(w):
            raw = keep.tile([P, PACK * w.shape[1]], F32, name="w_raw", tag="w_raw")
            nc.sync.dma_start(raw[:], w.rearrange("(p j) c -> p (j c)", j=PACK))
            return raw

        def entries(lst, first, count):
            return lst[:, first // 16 : (first + count) // 16]

        def quantise(grouped, name):
            width = grouped.shape[1] // PACK
            codes = keep.tile([P, width], U32, name=name + "_code", align_bytes=64)
            scales = keep.tile([P, width], U8, name=name + "_scale", align_bytes=64)
            nc.vector.quantize_mx(out=codes[:].bitcast(FP8X4), scales=scales[:], in_=grouped[:])
            return codes, scales

        def product(dst, lhs_codes, lhs_scales, rhs_codes, rhs_scales, factor):
            width = dst.shape[1]
            acc = psum.tile([P, BANK], F32, name="acc", tag="acc", bufs=3)
            nc.tensor.matmul_mx(out=acc[:, :width], lhsT=lhs_codes.bitcast(FP8X4), lhsT_scale=lhs_scales,
                                rhs=rhs_codes.bitcast(FP8X4), rhs_scale=rhs_scales, start=True, stop=True)
            nc.scalar.activation(dst, acc[:, :width], ACT.Copy, scale=factor)

        def bank(i):
            return psum.tile([P, BANK], F32, name="sums", tag="sums%d" % i)

        def blocks(width):
            return [slice(c, c + P) for c in range(0, width, P)]

        def add_turned(dst, terms):
            for i, term in enumerate(terms):
                nc.tensor.matmul(dst, term, ident[:], is_transpose=True, start=(i == 0), stop=(i == len(terms) - 1))

        scale_tab = keep.tile([P, T], U8, name="scale_tab")
        nc.vector.memset(scale_tab[:].bitcast(I32), 0)
        offs_l = load_list(offs, "offs_l")
        n1_l = load_list(n1, "n1_l")
        for q in range(4):
            nc.sync.dma_start(scale_tab[32 * q : 32 * q + 4, :].bitcast(I32), x_scales[0, 4 * q : 4 * q + 4, :].bitcast(I32))
        word_tab = keep.tile([P, T], I32, name="word_tab")
        nc.sync.dma_start(word_tab[:], x_words[0].rearrange("p n t -> p (n t)").bitcast(I32))
        w1_raw = load_weight(w1)
        gain = keep.tile([P, PACK], F32, name="gain")
        nc.sync.dma_start(gain[:], gn.rearrange("(p t) o -> p (t o)", t=PACK))
        n2_l = load_list(n2, "n2_l")
        n3_l = load_list(n3, "n3_l")
        n4_l = load_list(n4, "n4_l")

        ident = keep.tile([P, P], F32, name="ident")
        make_identity(nc, ident[:])
        gain4 = keep.tile([P, PACK], F32, name="gain4")
        nc.scalar.activation(gain4[:], gain[:], ACT.Copy, scale=4.0)

        x_scale = keep.tile([P, S], U8, name="x_scale", align_bytes=64)
        nc.vector.tensor_copy(x_scale[:], scale_tab[:].indirect(offs_l[:]))
        x_code = []
        for c in range(S // BANK):
            codes = keep.tile([P, BANK], U32, name="x_code%d" % c, align_bytes=64)
            nc.vector.tensor_copy(codes[:], word_tab[:].bitcast(U32).indirect(entries(offs_l, BANK * c, BANK)))
            x_code.append(codes)

        w1_b = [keep.tile([P, PACK * P], BF16, name="w1_b%d" % t, align_bytes=64) for t in range(PACK)]
        w1_cols = w1_raw[:].rearrange("p (j m t) -> p t m j", j=PACK, t=PACK)

        def deal_w1(copy, t):
            copy(w1_b[t][:].rearrange("p (m j) -> p m j", j=PACK), w1_cols[:, t])

        deal_w1(nc.vector.tensor_copy, 0)
        deal_w1(nc.scalar.copy, 1)
        w1_q = [quantise(w1_b[0], "w1q0")]
        for t in range(2, PACK):
            deal_w1(nc.vector.tensor_copy, t)
            w1_q.append(quantise(w1_b[t - 1], "w1q%d" % (t - 1)))
        w1_q.append(quantise(w1_b[PACK - 1], "w1q%d" % (PACK - 1)))
        w2_raw = load_weight(w2)

        rows = [keep.tile([P, S], F32, name="rows%d" % t) for t in range(PACK)]
        for t in range(PACK):
            for c in range(S // BANK):
                cols = slice(BANK * c, BANK * (c + 1))
                product(rows[t][:, cols], w1_q[t][0][:], w1_q[t][1][:], x_code[c][:], x_scale[:, cols], 0.25)

        def line_up(dst, t, v0, count):
            nc.vector.tensor_copy(dst, rows[t][:].indirect(entries(n1_l, 2 * v0, 2 * count)))

        def gained(dst, src, factors):
            nc.vector.tensor_tensor(dst.rearrange("p (v t) -> p v t", t=PACK), src.rearrange("p (t v) -> p v t", t=PACK),
                                    factors[:].unsqueeze(1).to_broadcast([P, P, PACK]), ALU.mult)

        def second_product(z_q, v0, count):
            for t, cols in enumerate(blocks(N)):
                product(rows[t][:, v0 : v0 + count], w2_q[0][:, cols], w2_q[1][:, cols], z_q[0][:], z_q[1][:], -0.5)

        w2_b = keep.tile([P, PACK * N], BF16, name="w2_b", align_bytes=64)
        parts = [(0, 2 * P), (2 * P, P)]
        turned = [bank(b) for b in range(EARLY // P)]
        for t in range(PACK):
            lined = [keep.tile([P, 2 * count], F32, name="lined%d_%d" % (t, v0)) for v0, count in parts]
            diff = [keep.tile([P, count], F32, name="diff", tag="diff%d_%d" % (t, v0)) for v0, count in parts]
            for i, (v0, count) in enumerate(parts):
                line_up(lined[i][:], t, v0, count)
            for i in range(len(parts)):
                nc.vector.tensor_tensor(diff[i][:], lined[i][:, 0::2], lined[i][:, 1::2], ALU.subtract)
            if t == 0:
                gaps = keep.tile([P, 2 * EARLY], F32, name="gaps_early")
            if t == 2:
                for c in range(4):
                    nc.scalar.copy(w2_b[:].rearrange("p (t m j) -> p m t j", t=PACK, j=PACK)[:, 32 * c : 32 * (c + 1)],
                                   w2_raw[:].rearrange("p (j m t) -> p m t j", j=PACK, t=PACK)[:, 32 * c : 32 * (c + 1)])
                gaps = keep.tile([P, 2 * EARLY], F32, name="gaps_late", tag="w_raw")
            gap = gaps[:, EARLY * (t % 2) : EARLY * (t % 2 + 1)]
            for i, (v0, count) in enumerate(parts):
                nc.scalar.activation(gap[:, v0 : v0 + count], diff[i][:], ACT.Abs, scale=3.0)
            for b, cols in enumerate(blocks(EARLY)):
                both = lined[b // 2][:, 2 * P * (b % 2) : 2 * P * (b % 2 + 1)]
                add_turned(turned[b][:, P * t : P * (t + 1)], [gap[:, cols], both[:, 0::2], both[:, 1::2]])
        back = []
        for b in range(EARLY // P):
            staged = keep.tile([P, BANK], F32, name="staged%d" % b)
            nc.scalar.copy(staged[:], turned[b][:])
            back.append(bank((len(turned) + b) % 5))
            for cols in blocks(BANK):
                nc.tensor.transpose(back[b][:, cols], staged[:, cols], ident[:])

        lined_late = keep.tile([P, 2 * P * PACK], F32, name="lined_late", tag="diff0_%d" % parts[1][0])
        for t in range(PACK):
            line_up(lined_late[:, 2 * P * t : 2 * P * (t + 1)], t, EARLY, P)
        w2_q = quantise(w2_b, "w2q")
        smaller = keep.tile([P, PACK * P], F32, name="smaller")
        nc.vector.tensor_tensor(smaller[:], lined_late[:, 0::2], lined_late[:, 1::2], ALU.min)
        larger = keep.tile([P, PACK * P], F32, name="larger")
        nc.vector.tensor_tensor(larger[:], lined_late[:, 0::2], lined_late[:, 1::2], ALU.max)
        z01 = keep.tile([P, 2 * BANK], BF16, name="z01", tag="z01", align_bytes=64)
        for b in range(2):
            gained(z01[:, BANK * b : BANK * (b + 1)], back[b][:], gain)
        z2 = keep.tile([P, BANK], BF16, name="z2", align_bytes=64)
        gained(z2[:], back[2][:], gain)
        second_product(quantise(z01, "z01q"), 0, 2 * P)
        mixed = keep.tile([P, PACK * P], F32, name="mixed", tag="z01", align_bytes=64)
        nc.vector.scalar_tensor_tensor(mixed[:], smaller[:], -0.5, larger[:], ALU.mult, ALU.add)
        second_product(quantise(z2, "z2q"), 2 * P, P)
        z3 = keep.tile([P, BANK], BF16, name="z3", align_bytes=64)
        gained(z3[:], mixed[:], gain4)
        second_product(quantise(z3, "z3q"), EARLY, P)

        out_rows = out.rearrange("(p t) v -> p t v", t=PACK)
        units = [(t, v0, HALF) for t in range(PACK - 1) for v0 in range(0, V, HALF)] + [(PACK - 1, 0, V)]

        def fresh(name, width):
            return keep.tile([P, width], F32, name=name, tag=name, bufs=len(units))

        def first_lookup(t, v0, count):
            p1 = fresh("p1", count)
            nc.vector.tensor_scalar(p1[:], rows[t][:].indirect(entries(n2_l, v0, count)), -1.0, 0.0, ALU.mult, ALU.add)
            return p1

        def lookup_plus(name, lst, p1, t, v0, count):
            total = fresh(name, count)
            nc.vector.tensor_tensor(total[:], rows[t][:].indirect(entries(lst, v0, count)), p1[:], ALU.add)
            return total

        def combine(name, in0, scalar, in1, op0, op1):
            res = fresh(name, in0.shape[1])
            nc.vector.scalar_tensor_tensor(res[:], in0[:], scalar, in1[:], op0, op1)
            return res

        def turned_sum(terms, i):
            acc = bank(i)
            for cols in blocks(HALF):
                add_turned(acc[:, cols], [term[:, cols] for term in terms])
            return acc[:, :HALF]

        p1_next = first_lookup(*units[0])
        for u, (t, v0, count) in enumerate(units[:-1]):
            p1 = p1_next
            e2 = lookup_plus("e2", n3_l, p1, t, v0, count)
            e3 = lookup_plus("e3", n4_l, p1, t, v0, count)
            p1_next = first_lookup(*units[u + 1])
            half = keep.tile([P, HALF], F32, name="half", tag="half")
            nc.scalar.activation(half[:], e2[:], ACT.Relu, scale=-1.0)
            lift = keep.tile([P, HALF], F32, name="lift", tag="lift")
            nc.scalar.activation(lift[:], e2[:], ACT.Relu, scale=-2.0)
            capped = combine("capped", e2, 0.0, e3, ALU.max, ALU.min)
            excess = fresh("excess", HALF)
            nc.scalar.activation(excess[:], turned_sum([half, e3], 0), ACT.Relu, scale=-3.0)
            rest = fresh("rest", HALF)
            nc.scalar.copy(rest[:], turned_sum([lift, p1, capped], 1))
            result = fresh("result", HALF)
            nc.scalar.copy(result[:], turned_sum([excess, rest], 2 + u % 2))
            nc.sync.dma_start(out_rows[:, t, v0 : v0 + HALF], result[:])

        t, v0, count = units[-1]
        p1 = p1_next
        e2 = lookup_plus("e2", n3_l, p1, t, v0, count)
        e3 = lookup_plus("e3", n4_l, p1, t, v0, count)
        over = combine("over", e2, 0.0, e3, ALU.min, ALU.subtract)
        base = combine("base", e3, -2.0, p1, ALU.mult, ALU.add)
        capped = combine("capped", e2, 0.0, e3, ALU.max, ALU.min)
        bent = combine("bent", over, -2.0, over, ALU.mult, ALU.max)
        halves = [slice(c, c + HALF) for c in range(0, V, HALF)]
        partial = [fresh("partial", HALF) for cols in halves]
        for i, cols in enumerate(halves):
            nc.vector.tensor_tensor(partial[i][:], base[:, cols], capped[:, cols], ALU.add)
        for i, cols in enumerate(halves):
            result = fresh("last_result", HALF)
            nc.vector.tensor_tensor(result[:], partial[i][:], bent[:, cols], ALU.add)
            nc.sync.dma_start(out_rows[:, t, cols], result[:])
